import numpy as np, ml_dtypes
CORES = [12,28,44,60,3,19,35,51]
N = 8
S, B = 3, 128
def setup_inputs(rng):
    a = (rng.standard_normal((128, 128), dtype=np.float32) / 12).astype(ml_dtypes.bfloat16)
    return {"x": rng.standard_normal((N, 128, S * B), dtype=np.float32).astype(ml_dtypes.bfloat16), "a": np.broadcast_to(a, (N, 128, 128)).copy(), "at": np.broadcast_to(a.T, (N, 128, 128)).copy()}
def setup_inputs_big(rng):
    d = setup_inputs(rng)
    for k in ("x",): d[k] = (d[k].astype(np.float32) * 1048576.0).astype(d[k].dtype)
    return d
def setup_inputs_small(rng):
    d = setup_inputs(rng)
    for k in ("x",): d[k] = (d[k].astype(np.float32) * (1 / 1048576.0)).astype(d[k].dtype)
    return d
def setup_inputs_apart(rng):
    d = setup_inputs(rng)
    f = (10.0 ** rng.permutation(np.linspace(-1.5, 1.5, N))).astype(np.float32).reshape(N, 1, 1)
    for k in ("x",): d[k] = (d[k].astype(np.float32) * f).astype(d[k].dtype)
    return d
def reference(x, a, at):
    X, A = x.astype(np.float64), a.astype(np.float64)
    y = np.zeros((N, 128, S * B)); h = np.zeros((128, B))
    for r in range(N):
        for s in range(S):
            h = A[r].T @ h + X[r][:, B * s:B * s + B]
            y[r][:, B * s:B * s + B] = h
    return {"y": y.astype(ml_dtypes.bfloat16)}

@@ -1,0 +1,265 @@
+from concourse.bass import DstId, RemoteDMATransfer
+from concourse.mybir import dt, AluOpType
+
+P = 128
+NR = 8
+S = 3
+MAXPOW = S * (NR - 1)
+NBANK = 4
+
+RELAY_IN_ENGINES = 16
+RELAY_OUT_ENGINES = 8
+DIRECT_ENGINES = 8
+
+SCRATCH = {
+    "xb": ("sbuf", [P, S * P], "bfloat16"),
+    "pw": ("sbuf", [P, MAXPOW * P], "bfloat16"),
+    "atp": ("sbuf", [P, 5 * P], "bfloat16"),
+    "lc": ("sbuf", [P, 2 * P], "bfloat16"),
+    "land": ("sbuf", [P, (NR - 1) * P], "bfloat16"),
+    "yb": ("sbuf", [P, S * P], "bfloat16"),
+    "py0": ("psum", [P, 512], "float32"),
+    "py1": ("psum", [P, 512], "float32"),
+    "py2": ("psum", [P, 512], "float32"),
+    "ph": ("psum", [P, 512], "float32"),
+    "pp0": ("psum", [P, 512], "float32"),
+    "pp1": ("psum", [P, 512], "float32"),
+    "pp2": ("psum", [P, 512], "float32"),
+    "pp3": ("psum", [P, 512], "float32"),
+}
+PSUM = ("py0", "py1", "py2", "ph", "pp0", "pp1", "pp2", "pp3")
+SEMAPHORES = ["ldx", "lda", "ldat", "pe", "dve", "sent", "st", "st2"] + ["arr%d" % j for j in range(NR - 1)]
+
+
+def _pick(mask, k):
+    bits = [i for i in range(mask.bit_length()) if (mask >> i) & 1][:k]
+    return sum(1 << i for i in bits)
+
+
+def _count(mask):
+    return sum((mask >> i) & 1 for i in range(mask.bit_length()))
+
+
+def _common_mask(topo, src, dsts, k):
+    m = topo.mask(src, dsts[0])
+    for d in dsts[1:]:
+        m &= topo.mask(src, d)
+    return _pick(m, k)
+
+
+def _plan(T, topo):
+    cores = list(T.cores)
+    n = len(cores)
+    direct, far = {}, {}
+    for j, c in enumerate(cores):
+        direct[j] = [r for r in range(j + 1, n) if topo.may_write(c, cores[r])]
+        away = [r for r in range(j + 1, n) if not topo.may_write(c, cores[r])]
+        first = [i for i, r in enumerate(away) if topo.mates(topo.chip(c), topo.chip(cores[r]))]
+        if first:
+            away = away[first[0]:] + away[:first[0]]
+        cands = [k for k in range(topo.CORES_PER_CHIP * topo.CHIPS)
+                 if topo.chip(k) == topo.chip(c) and k not in cores
+                 and all(topo.may_write(k, cores[r]) for r in away)]
+        cands.sort(key=lambda k: (topo.die(k) != topo.die(c), k))
+        far[j] = [(cands[i % len(cands)], r) for i, r in enumerate(away)]
+    return cores, direct, far
+
+
+def _dst(topo, c):
+    rid, pid, _se = topo.addr(c)
+    return DstId(rid=rid, pnc=pid)
+
+
+def rank_program(g, core, T, topo):
+    cores, direct, far = _plan(T, topo)
+
+    def slot(j):
+        return T.land[:, j * P:(j + 1) * P]
+
+    def relay_in_mask(j):
+        return _common_mask(topo, cores[j], sorted(set(h for h, _r in far[j])), RELAY_IN_ENGINES)
+
+    def relay_out_mask(h, r):
+        return _pick(topo.mask(h, cores[r]), RELAY_OUT_ENGINES)
+
+    def direct_mask(j):
+        return _common_mask(topo, cores[j], [cores[r] for r in direct[j]], DIRECT_ENGINES)
+
+    rank = T.rank_of(core)
+    if rank is None:
+        sent = 0
+        for j in range(len(cores)):
+            mine = [r for h, r in far[j] if h == core]
+            if not mine:
+                continue
+            g.wait_ge(T.sem["arr%d" % j], _count(relay_in_mask(j)))
+            for r in mine:
+                rid, pid, _se = topo.addr(cores[r])
+                m = relay_out_mask(core, r)
+                g.remote_dma(slot(j), slot(j), T.sem["arr%d" % j], T.sem.sent, pid, rid, m)
+                sent += _count(m)
+        if sent:
+            g.wait_ge(T.sem.sent, sent)
+        return
+
+    Q = {"pe": g.tensor, "dve": g.vector, "g": g, "sync": g.sync, "scalar": g.scalar}
+    seen, count, log = {}, {"pe": 0, "dve": 0}, []
+
+    def ap(t):
+        return T[t[0]][:, t[1]:t[2]]
+
+    def need(q, sem, val):
+        if seen.get((q, sem), 0) < val:
+            Q[q].wait_ge(T.sem[sem], val)
+            seen[(q, sem)] = val
+
+    def order(q, reads, writes):
+        want = {}
+        for is_w, lst in ((False, reads), (True, writes)):
+            for buf, lo, hi in lst:
+                for b, l, h, w, oq, sem, val in log:
+                    if b != buf:
+                        continue
+                    if buf in PSUM:
+                        hit = oq != q
+                    else:
+                        hit = l < hi and lo < h and ((not is_w and w) or (is_w and oq != q))
+                    if hit:
+                        want[sem] = max(want.get(sem, 0), val)
+        for sem in sorted(want):
+            need(q, sem, want[sem])
+
+    def note(q, reads, writes, sem, val):
+        for buf, lo, hi in reads:
+            log.append((buf, lo, hi, False, q, sem, val))
+        for buf, lo, hi in writes:
+            log.append((buf, lo, hi, True, q, sem, val))
+
+    def mm(out, lhsT, rhs, start, stop):
+        order("pe", [lhsT, rhs], [out])
+        count["pe"] += 1
+        g.tensor.matmul(ap(out), ap(lhsT), ap(rhs), start, stop).then_inc(T.sem.pe, 1)
+        note("pe", [lhsT, rhs], [out], "pe", count["pe"])
+
+    def add(out, in0, in1):
+        order("dve", [in0, in1], [out])
+        count["dve"] += 1
+        g.vector.tensor_tensor(ap(out), ap(in0), ap(in1), AluOpType.add).then_inc(T.sem.dve, 1)
+        note("dve", [in0, in1], [out], "dve", count["dve"])
+
+    def copy(out, in_):
+        order("dve", [in_], [out])
+        count["dve"] += 1
+        g.vector.tensor_copy(ap(out), ap(in_)).then_inc(T.sem.dve, 1)
+        note("dve", [in_], [out], "dve", count["dve"])
+
+    def apow(k, k2=None):
+        return ("pw", (k - 1) * P, (k2 or k) * P)
+
+    def atpow(m):
+        i = m.bit_length() - 1
+        return ("atp", i * P, (i + 1) * P)
+
+    def xs(s):
+        return ("xb", s * P, (s + 1) * P)
+
+    L1, C = ("lc", 0, P), ("lc", P, 2 * P)
+    npow = S * rank
+
+    g.sync.dma_start(T.xb[:], T.x[:]).then_inc(T.sem.ldx, 16)
+    note("dma", [], [("xb", 0, S * P)], "ldx", 16)
+    g.scalar.dma_start(ap(apow(1)), T.a[:]).then_inc(T.sem.lda, 16)
+    note("dma", [], [apow(1)], "lda", 16)
+    if npow > 1:
+        g.scalar.dma_start(ap(atpow(1)), T.at[:]).then_inc(T.sem.ldat, 16)
+        note("dma", [], [atpow(1)], "ldat", 16)
+
+    sources = []
+    for j in range(rank):
+        if rank in direct[j]:
+            sources.append((0, direct[j].index(rank), j, _count(direct_mask(j))))
+        else:
+            pos = [i for i, (h, r) in enumerate(far[j]) if r == rank][0]
+            sources.append((1, pos, j, _count(relay_out_mask(far[j][pos][0], rank))))
+    sources.sort()
+    for _k, _p, j, n_eng in sources:
+        note("remote", [], [("land", j * P, (j + 1) * P)], "arr%d" % j, n_eng)
+
+    levels, m, nb = [], 1, 0
+    while m < npow:
+        lev = []
+        if npow > 2 * m:
+            lev.append((("pp%d" % (nb % NBANK), 0, P), atpow(2 * m), apow(m), atpow(m)))
+            nb += 1
+        k = m + 1
+        while k <= min(2 * m, npow):
+            k2 = min(k + 3, 2 * m, npow)
+            lev.append((("pp%d" % (nb % NBANK), 0, (k2 - k + 1) * P), apow(k, k2), atpow(m), apow(k - m, k2 - m)))
+            nb += 1
+            k = k2 + 1
+        levels.append(lev)
+        m *= 2
+
+    def level_mm(lev):
+        for ps, _sb, lhsT, rhs in lev:
+            mm(ps, lhsT, rhs, True, True)
+
+    def level_copy(lev):
+        for ps, sb, _lhsT, _rhs in lev:
+            copy(sb, ps)
+
+    urgent = bool(far[rank])
+    mm(("ph", 0, P), apow(1), xs(0), True, True)
+    if levels and not urgent:
+        level_mm(levels[0])
+    add(L1, ("ph", 0, P), xs(1))
+    if levels and not urgent:
+        level_copy(levels[0])
+        levels = levels[1:]
+    mm(("ph", P, 2 * P), apow(1), L1, True, True)
+    add(C, ("ph", P, 2 * P), xs(2))
+
+    sent = 0
+    if far[rank] or direct[rank]:
+        order("g", [C], [])
+    if far[rank]:
+        m1 = relay_in_mask(rank)
+        hs = []
+        for h, _r in far[rank]:
+            if h not in hs:
+                hs.append(h)
+        g.remote_dma_fused([RemoteDMATransfer(dst_ids=[_dst(topo, h) for h in hs], dma_engine_mask=m1,
+                                              remote_sem=T.sem["arr%d" % rank], srcs=[ap(C)],
+                                              dsts=[slot(rank) for _h in hs])], local_sem=T.sem.sent)
+        sent += _count(m1)
+    if direct[rank]:
+        m2 = direct_mask(rank)
+        g.remote_dma_fused([RemoteDMATransfer(dst_ids=[_dst(topo, cores[r]) for r in direct[rank]],
+                                              dma_engine_mask=m2, remote_sem=T.sem["arr%d" % rank], srcs=[ap(C)],
+                                              dsts=[slot(rank) for _r in direct[rank]])], local_sem=T.sem.sent)
+        sent += _count(m2)
+
+    for lev in levels:
+        level_mm(lev)
+        level_copy(lev)
+
+    if rank == 0:
+        order("sync", [xs(0)], [])
+        g.sync.dma_start(T.y[:, 0:P], ap(xs(0))).then_inc(T.sem.st, 16)
+        order("scalar", [L1, C], [])
+        g.scalar.dma_start(T.y[:, P:S * P], T.lc[:]).then_inc(T.sem.st2, 16)
+        g.sync.wait_ge(T.sem.st, 16)
+        g.scalar.wait_ge(T.sem.st2, 16)
+    else:
+        for i, (_k, _p, j, _n) in enumerate(sources):
+            for s in range(S):
+                mm(("py%d" % s, 0, P), apow(s + 1 + S * (rank - 1 - j)), ("land", j * P, (j + 1) * P),
+                   i == 0, i == len(sources) - 1)
+        loc = (xs(0), L1, C)
+        for s in range(S):
+            add(("yb", s * P, (s + 1) * P), ("py%d" % s, 0, P), loc[s])
+        order("sync", [("yb", 0, S * P)], [])
+        g.sync.dma_start(T.y[:], T.yb[:]).then_inc(T.sem.st, 16)
+        g.sync.wait_ge(T.sem.st, 16)
+    if sent:
+        g.wait_ge(T.sem.sent, sent)

@@ -4,21 +4,24 @@ from concourse.mybir import dt, AluOpType
 P = 128
 NR = 8
 S = 3
-MAXPOW = S * (NR - 1)
 NBANK = 4
 
 RELAY_IN_ENGINES = 16
 RELAY_OUT_ENGINES = 8
 DIRECT_ENGINES = 8
+EW = 64
 
 SCRATCH = {
     "xb": ("sbuf", [P, S * P], "bfloat16"),
-    "pw": ("sbuf", [P, MAXPOW * P], "bfloat16"),
+    "q": ("sbuf", [P, (NR - 1) * P], "bfloat16"),
+    "ap": ("sbuf", [P, 3 * P], "bfloat16"),
     "atp": ("sbuf", [P, 5 * P], "bfloat16"),
-    "lc": ("sbuf", [P, 2 * P], "bfloat16"),
+    "lc": ("sbuf", [P, 3 * P], "bfloat16"),
     "land": ("sbuf", [P, (NR - 1) * P], "bfloat16"),
+    "landx": ("sbuf", [P, (NR - 1) * P], "bfloat16"),
+    "hb": ("sbuf", [P, P], "bfloat16"),
     "yb": ("sbuf", [P, S * P], "bfloat16"),
-    "py0": ("psum", [P, 512], "float32"),
+    "pH": ("psum", [P, 512], "float32"),
     "py1": ("psum", [P, 512], "float32"),
     "py2": ("psum", [P, 512], "float32"),
     "ph": ("psum", [P, 512], "float32"),
@@ -27,8 +30,9 @@ SCRATCH = {
     "pp2": ("psum", [P, 512], "float32"),
     "pp3": ("psum", [P, 512], "float32"),
 }
-PSUM = ("py0", "py1", "py2", "ph", "pp0", "pp1", "pp2", "pp3")
-SEMAPHORES = ["ldx", "lda", "ldat", "pe", "dve", "sent", "st", "st2"] + ["arr%d" % j for j in range(NR - 1)]
+PSUM = ("pH", "py1", "py2", "ph", "pp0", "pp1", "pp2", "pp3")
+SEMAPHORES = (["ldx", "ldx2", "lda", "ldat", "pe", "dve", "sent", "st", "st2"]
+              + ["arr%d" % j for j in range(NR - 1)] + ["arx%d" % j for j in range(NR - 1)])
 
 
 def _pick(mask, k):
@@ -54,9 +58,9 @@ def _plan(T, topo):
     for j, c in enumerate(cores):
         direct[j] = [r for r in range(j + 1, n) if topo.may_write(c, cores[r])]
         away = [r for r in range(j + 1, n) if not topo.may_write(c, cores[r])]
-        first = [i for i, r in enumerate(away) if topo.mates(topo.chip(c), topo.chip(cores[r]))]
-        if first:
-            away = away[first[0]:] + away[:first[0]]
+        mate = [i for i, r in enumerate(away) if topo.mates(topo.chip(c), topo.chip(cores[r]))]
+        if mate:
+            away = away[mate[0] + 1:] + away[:mate[0] + 1]
         cands = [k for k in range(topo.CORES_PER_CHIP * topo.CHIPS)
                  if topo.chip(k) == topo.chip(c) and k not in cores
                  and all(topo.may_write(k, cores[r]) for r in away)]
@@ -73,17 +77,21 @@ def _dst(topo, c):
 def rank_program(g, core, T, topo):
     cores, direct, far = _plan(T, topo)
 
-    def slot(j):
-        return T.land[:, j * P:(j + 1) * P]
-
     def relay_in_mask(j):
         return _common_mask(topo, cores[j], sorted(set(h for h, _r in far[j])), RELAY_IN_ENGINES)
 
-    def relay_out_mask(h, r):
-        return _pick(topo.mask(h, cores[r]), RELAY_OUT_ENGINES)
+    def relay_out_mask(h, rs):
+        return _common_mask(topo, h, [cores[r] for r in rs], RELAY_OUT_ENGINES)
 
     def direct_mask(j):
         return _common_mask(topo, cores[j], [cores[r] for r in direct[j]], DIRECT_ENGINES)
+
+    def send(src, dst_cores, mask, buf, sem, j, lo=0):
+        g.remote_dma_fused([RemoteDMATransfer(dst_ids=[_dst(topo, d) for d in dst_cores], dma_engine_mask=mask,
+                                              remote_sem=T.sem["%s%d" % (sem, j)], srcs=[src],
+                                              dsts=[T[buf][:, j * P + lo:(j + 1) * P] for _d in dst_cores])],
+                           local_sem=T.sem.sent)
+        return _count(mask)
 
     rank = T.rank_of(core)
     if rank is None:
@@ -92,18 +100,16 @@ def rank_program(g, core, T, topo):
             mine = [r for h, r in far[j] if h == core]
             if not mine:
                 continue
-            g.wait_ge(T.sem["arr%d" % j], _count(relay_in_mask(j)))
-            for r in mine:
-                rid, pid, _se = topo.addr(cores[r])
-                m = relay_out_mask(core, r)
-                g.remote_dma(slot(j), slot(j), T.sem["arr%d" % j], T.sem.sent, pid, rid, m)
-                sent += _count(m)
+            for buf, sem, lo in (("landx", "arx", P - EW), ("land", "arr", 0)):
+                g.wait_ge(T.sem["%s%d" % (sem, j)], _count(relay_in_mask(j)))
+                sent += send(T[buf][:, j * P + lo:(j + 1) * P], [cores[r] for r in mine], relay_out_mask(core, mine),
+                             buf, sem, j, lo)
         if sent:
             g.wait_ge(T.sem.sent, sent)
         return
 
     Q = {"pe": g.tensor, "dve": g.vector, "g": g, "sync": g.sync, "scalar": g.scalar}
-    seen, count, log = {}, {"pe": 0, "dve": 0}, []
+    seen, count, log, pending = {}, {"pe": 0, "dve": 0}, [], []
 
     def ap(t):
         return T[t[0]][:, t[1]:t[2]]
@@ -135,7 +141,23 @@ def rank_program(g, core, T, topo):
         for buf, lo, hi in writes:
             log.append((buf, lo, hi, True, q, sem, val))
 
+    def copy(out, in_):
+        order("dve", [in_], [out])
+        count["dve"] += 1
+        g.vector.tensor_copy(ap(out), ap(in_)).then_inc(T.sem.dve, 1)
+        note("dve", [in_], [out], "dve", count["dve"])
+
+    def flush(n):
+        for ps, sb in pending[:n]:
+            copy(sb, ps)
+        del pending[:n]
+
     def mm(out, lhsT, rhs, start, stop):
+        n = 0
+        for i, (ps, sb) in enumerate(pending):
+            if ps[0] == out[0] or any(sb[0] == t[0] and sb[1] < t[2] and t[1] < sb[2] for t in (lhsT, rhs)):
+                n = i + 1
+        flush(n)
         order("pe", [lhsT, rhs], [out])
         count["pe"] += 1
         g.tensor.matmul(ap(out), ap(lhsT), ap(rhs), start, stop).then_inc(T.sem.pe, 1)
@@ -147,118 +169,125 @@ def rank_program(g, core, T, topo):
         g.vector.tensor_tensor(ap(out), ap(in0), ap(in1), AluOpType.add).then_inc(T.sem.dve, 1)
         note("dve", [in0, in1], [out], "dve", count["dve"])
 
-    def copy(out, in_):
-        order("dve", [in_], [out])
+    def zero(out):
+        order("dve", [], [out])
         count["dve"] += 1
-        g.vector.tensor_copy(ap(out), ap(in_)).then_inc(T.sem.dve, 1)
-        note("dve", [in_], [out], "dve", count["dve"])
+        g.vector.memset(ap(out), 0.0).then_inc(T.sem.dve, 1)
+        note("dve", [], [out], "dve", count["dve"])
 
-    def apow(k, k2=None):
-        return ("pw", (k - 1) * P, (k2 or k) * P)
+    def load(queue, out, in_, sem):
+        queue.dma_start(ap(out), in_).then_inc(T.sem[sem], 16)
+        note("dma", [], [out], sem, 16)
 
-    def atpow(m):
-        i = m.bit_length() - 1
-        return ("atp", i * P, (i + 1) * P)
+    def blk(buf, i, n=1):
+        return (buf, i * P, (i + n) * P)
 
-    def xs(s):
-        return ("xb", s * P, (s + 1) * P)
+    A1, A2, A3, A6 = blk("q", 0), blk("ap", 0), blk("ap", 1), blk("ap", 2)
+    AT1, AT2, AT3, AT6, AT12 = (blk("atp", i) for i in range(5))
+    L1, C, V = blk("lc", 0), blk("lc", 1), blk("lc", 2)
+    AHEAD = ("xb", S * P - EW, S * P)
+    urgent = bool(far[rank])
 
-    L1, C = ("lc", 0, P), ("lc", P, 2 * P)
-    npow = S * rank
-
-    g.sync.dma_start(T.xb[:], T.x[:]).then_inc(T.sem.ldx, 16)
-    note("dma", [], [("xb", 0, S * P)], "ldx", 16)
-    g.scalar.dma_start(ap(apow(1)), T.a[:]).then_inc(T.sem.lda, 16)
-    note("dma", [], [apow(1)], "lda", 16)
-    if npow > 1:
-        g.scalar.dma_start(ap(atpow(1)), T.at[:]).then_inc(T.sem.ldat, 16)
-        note("dma", [], [atpow(1)], "ldat", 16)
+    if urgent:
+        load(g.sync, AHEAD, T.x[:, S * P - EW:S * P], "ldx2")
+        load(g.scalar, A1, T.a[:], "lda")
+        load(g.sync, ("xb", 0, S * P - EW), T.x[:, 0:S * P - EW], "ldx")
+        if rank:
+            load(g.sync, AT1, T.at[:], "ldat")
+    else:
+        load(g.sync, blk("xb", 0, 3), T.x[:], "ldx")
+        load(g.scalar, A1, T.a[:], "lda")
+        load(g.scalar, AT1, T.at[:], "ldat")
 
     sources = []
     for j in range(rank):
         if rank in direct[j]:
-            sources.append((0, direct[j].index(rank), j, _count(direct_mask(j))))
+            sources.append((0, direct[j].index(rank), "land", j))
+            note("remote", [], [blk("land", j)], "arr%d" % j, _count(direct_mask(j)))
         else:
             pos = [i for i, (h, r) in enumerate(far[j]) if r == rank][0]
-            sources.append((1, pos, j, _count(relay_out_mask(far[j][pos][0], rank))))
+            h = far[j][pos][0]
+            n_eng = _count(relay_out_mask(h, [r for hh, r in far[j] if hh == h]))
+            sources.append((1, pos, "landx", j))
+            sources.append((2, pos, "land", j))
+            note("remote", [], [("landx", (j + 1) * P - EW, (j + 1) * P)], "arx%d" % j, n_eng)
+            zero(("landx", j * P, (j + 1) * P - EW))
+            note("remote", [], [blk("land", j)], "arr%d" % j, n_eng)
     sources.sort()
-    for _k, _p, j, n_eng in sources:
-        note("remote", [], [("land", j * P, (j + 1) * P)], "arr%d" % j, n_eng)
 
-    levels, m, nb = [], 1, 0
-    while m < npow:
-        lev = []
-        if npow > 2 * m:
-            lev.append((("pp%d" % (nb % NBANK), 0, P), atpow(2 * m), apow(m), atpow(m)))
-            nb += 1
-        k = m + 1
-        while k <= min(2 * m, npow):
-            k2 = min(k + 3, 2 * m, npow)
-            lev.append((("pp%d" % (nb % NBANK), 0, (k2 - k + 1) * P), apow(k, k2), atpow(m), apow(k - m, k2 - m)))
-            nb += 1
-            k = k2 + 1
-        levels.append(lev)
-        m *= 2
+    tasks = []
+    if rank >= 1:
+        tasks.append((A2, AT1, A1))
+    if rank >= 2:
+        tasks = [(AT2, A1, AT1), (A2, AT1, A1), (AT3, A1, AT2)]
+        if rank >= 3:
+            tasks.append((A3, AT1, A2))
+            tasks.append((AT6, A3, AT3))
+        tasks.append((blk("q", 1), AT3, A1))
+        if rank >= 5:
+            tasks.append((A6, AT3, A3))
+        if rank >= 3:
+            tasks.append((blk("q", 2, min(rank, 4) - 2), AT6, blk("q", 0, min(rank, 4) - 2)))
+        if rank >= 5:
+            tasks.append((AT12, A6, AT6))
+            tasks.append((blk("q", 4, rank - 4), AT12, blk("q", 0, rank - 4)))
+    nb = [0]
 
-    def level_mm(lev):
-        for ps, _sb, lhsT, rhs in lev:
-            mm(ps, lhsT, rhs, True, True)
+    def power(t):
+        ps = ("pp%d" % (nb[0] % NBANK), 0, t[0][2] - t[0][1])
+        nb[0] += 1
+        mm(ps, t[1], t[2], True, True)
+        pending.append((ps, t[0]))
 
-    def level_copy(lev):
-        for ps, sb, _lhsT, _rhs in lev:
-            copy(sb, ps)
-
-    urgent = bool(far[rank])
-    mm(("ph", 0, P), apow(1), xs(0), True, True)
-    if levels and not urgent:
-        level_mm(levels[0])
-    add(L1, ("ph", 0, P), xs(1))
-    if levels and not urgent:
-        level_copy(levels[0])
-        levels = levels[1:]
-    mm(("ph", P, 2 * P), apow(1), L1, True, True)
-    add(C, ("ph", P, 2 * P), xs(2))
+    mm(("ph", 0, P), A1, blk("xb", 0), True, True)
+    if not urgent:
+        for t in tasks[:2]:
+            power(t)
+        tasks = tasks[2:]
+    add(L1, ("ph", 0, P), blk("xb", 1))
+    flush(len(pending))
+    mm(("ph", P, 2 * P), A1, L1, True, True)
+    if urgent:
+        add(("lc", 2 * P, 3 * P - EW), ("ph", P, 2 * P - EW), ("xb", 2 * P, 3 * P - EW))
+        copy(("lc", 3 * P - EW, 3 * P), ("ph", 2 * P - EW, 2 * P))
+    add(C, ("ph", P, 2 * P), blk("xb", 2))
 
     sent = 0
-    if far[rank] or direct[rank]:
-        order("g", [C], [])
     if far[rank]:
-        m1 = relay_in_mask(rank)
         hs = []
         for h, _r in far[rank]:
             if h not in hs:
                 hs.append(h)
-        g.remote_dma_fused([RemoteDMATransfer(dst_ids=[_dst(topo, h) for h in hs], dma_engine_mask=m1,
-                                              remote_sem=T.sem["arr%d" % rank], srcs=[ap(C)],
-                                              dsts=[slot(rank) for _h in hs])], local_sem=T.sem.sent)
-        sent += _count(m1)
+        order("g", [AHEAD], [])
+        sent += send(ap(AHEAD), hs, relay_in_mask(rank), "landx", "arx", rank, P - EW)
+        order("g", [V], [])
+        sent += send(ap(V), hs, relay_in_mask(rank), "land", "arr", rank)
     if direct[rank]:
-        m2 = direct_mask(rank)
-        g.remote_dma_fused([RemoteDMATransfer(dst_ids=[_dst(topo, cores[r]) for r in direct[rank]],
-                                              dma_engine_mask=m2, remote_sem=T.sem["arr%d" % rank], srcs=[ap(C)],
-                                              dsts=[slot(rank) for _r in direct[rank]])], local_sem=T.sem.sent)
-        sent += _count(m2)
+        order("g", [C], [])
+        sent += send(ap(C), [cores[r] for r in direct[rank]], direct_mask(rank), "land", "arr", rank)
 
-    for lev in levels:
-        level_mm(lev)
-        level_copy(lev)
+    for t in tasks:
+        power(t)
+    flush(len(pending))
 
     if rank == 0:
-        order("sync", [xs(0)], [])
-        g.sync.dma_start(T.y[:, 0:P], ap(xs(0))).then_inc(T.sem.st, 16)
+        order("sync", [blk("xb", 0)], [])
+        g.sync.dma_start(T.y[:, 0:P], ap(blk("xb", 0))).then_inc(T.sem.st, 16)
         order("scalar", [L1, C], [])
-        g.scalar.dma_start(T.y[:, P:S * P], T.lc[:]).then_inc(T.sem.st2, 16)
+        g.scalar.dma_start(T.y[:, P:S * P], T.lc[:, 0:2 * P]).then_inc(T.sem.st2, 16)
         g.sync.wait_ge(T.sem.st, 16)
         g.scalar.wait_ge(T.sem.st2, 16)
     else:
-        for i, (_k, _p, j, _n) in enumerate(sources):
-            for s in range(S):
-                mm(("py%d" % s, 0, P), apow(s + 1 + S * (rank - 1 - j)), ("land", j * P, (j + 1) * P),
-                   i == 0, i == len(sources) - 1)
-        loc = (xs(0), L1, C)
-        for s in range(S):
-            add(("yb", s * P, (s + 1) * P), ("py%d" % s, 0, P), loc[s])
-        order("sync", [("yb", 0, S * P)], [])
+        PH, HB = ("pH", 0, P), ("hb", 0, P)
+        for i, (_k, _p, buf, j) in enumerate(sources):
+            mm(PH, blk("q", rank - 1 - j), blk(buf, j), i == 0, i == len(sources) - 1)
+        copy(HB, PH)
+        mm(("py1", 0, P), A1, HB, True, True)
+        mm(("py2", 0, P), A2, HB, True, True)
+        add(blk("yb", 0), PH, blk("xb", 0))
+        add(blk("yb", 1), ("py1", 0, P), L1)
+        add(blk("yb", 2), ("py2", 0, P), C)
+        order("sync", [blk("yb", 0, 3)], [])
         g.sync.dma_start(T.y[:], T.yb[:]).then_inc(T.sem.st, 16)
         g.sync.wait_ge(T.sem.st, 16)
     if sent:

from concourse.bass import DstId, RemoteDMATransfer
from concourse.mybir import dt, AluOpType

P = 128
NR = 8
S = 3
NBANK = 4

RELAY_IN_ENGINES = 16
RELAY_OUT_ENGINES = 8
DIRECT_ENGINES = 8
EW = 64

SCRATCH = {
    "xb": ("sbuf", [P, S * P], "bfloat16"),
    "q": ("sbuf", [P, (NR - 1) * P], "bfloat16"),
    "ap": ("sbuf", [P, 3 * P], "bfloat16"),
    "atp": ("sbuf", [P, 5 * P], "bfloat16"),
    "lc": ("sbuf", [P, 3 * P], "bfloat16"),
    "land": ("sbuf", [P, (NR - 1) * P], "bfloat16"),
    "landx": ("sbuf", [P, (NR - 1) * P], "bfloat16"),
    "hb": ("sbuf", [P, P], "bfloat16"),
    "yb": ("sbuf", [P, S * P], "bfloat16"),
    "pH": ("psum", [P, 512], "float32"),
    "py1": ("psum", [P, 512], "float32"),
    "py2": ("psum", [P, 512], "float32"),
    "ph": ("psum", [P, 512], "float32"),
    "pp0": ("psum", [P, 512], "float32"),
    "pp1": ("psum", [P, 512], "float32"),
    "pp2": ("psum", [P, 512], "float32"),
    "pp3": ("psum", [P, 512], "float32"),
}
PSUM = ("pH", "py1", "py2", "ph", "pp0", "pp1", "pp2", "pp3")
SEMAPHORES = (["ldx", "ldx2", "lda", "ldat", "pe", "dve", "sent", "st", "st2"]
              + ["arr%d" % j for j in range(NR - 1)] + ["arx%d" % j for j in range(NR - 1)])


def _pick(mask, k):
    bits = [i for i in range(mask.bit_length()) if (mask >> i) & 1][:k]
    return sum(1 << i for i in bits)


def _count(mask):
    return sum((mask >> i) & 1 for i in range(mask.bit_length()))


def _common_mask(topo, src, dsts, k):
    m = topo.mask(src, dsts[0])
    for d in dsts[1:]:
        m &= topo.mask(src, d)
    return _pick(m, k)


def _plan(T, topo):
    cores = list(T.cores)
    n = len(cores)
    direct, far = {}, {}
    for j, c in enumerate(cores):
        direct[j] = [r for r in range(j + 1, n) if topo.may_write(c, cores[r])]
        away = [r for r in range(j + 1, n) if not topo.may_write(c, cores[r])]
        mate = [i for i, r in enumerate(away) if topo.mates(topo.chip(c), topo.chip(cores[r]))]
        if mate:
            away = away[mate[0] + 1:] + away[:mate[0] + 1]
        cands = [k for k in range(topo.CORES_PER_CHIP * topo.CHIPS)
                 if topo.chip(k) == topo.chip(c) and k not in cores
                 and all(topo.may_write(k, cores[r]) for r in away)]
        cands.sort(key=lambda k: (topo.die(k) != topo.die(c), k))
        far[j] = [(cands[i % len(cands)], r) for i, r in enumerate(away)]
    return cores, direct, far


def _dst(topo, c):
    rid, pid, _se = topo.addr(c)
    return DstId(rid=rid, pnc=pid)


def rank_program(g, core, T, topo):
    cores, direct, far = _plan(T, topo)

    def relay_in_mask(j):
        return _common_mask(topo, cores[j], sorted(set(h for h, _r in far[j])), RELAY_IN_ENGINES)

    def relay_out_mask(h, rs):
        return _common_mask(topo, h, [cores[r] for r in rs], RELAY_OUT_ENGINES)

    def direct_mask(j):
        return _common_mask(topo, cores[j], [cores[r] for r in direct[j]], DIRECT_ENGINES)

    def send(src, dst_cores, mask, buf, sem, j, lo=0):
        g.remote_dma_fused([RemoteDMATransfer(dst_ids=[_dst(topo, d) for d in dst_cores], dma_engine_mask=mask,
                                              remote_sem=T.sem["%s%d" % (sem, j)], srcs=[src],
                                              dsts=[T[buf][:, j * P + lo:(j + 1) * P] for _d in dst_cores])],
                           local_sem=T.sem.sent)
        return _count(mask)

    rank = T.rank_of(core)
    if rank is None:
        sent = 0
        for j in range(len(cores)):
            mine = [r for h, r in far[j] if h == core]
            if not mine:
                continue
            for buf, sem, lo in (("landx", "arx", P - EW), ("land", "arr", 0)):
                g.wait_ge(T.sem["%s%d" % (sem, j)], _count(relay_in_mask(j)))
                sent += send(T[buf][:, j * P + lo:(j + 1) * P], [cores[r] for r in mine], relay_out_mask(core, mine),
                             buf, sem, j, lo)
        if sent:
            g.wait_ge(T.sem.sent, sent)
        return

    Q = {"pe": g.tensor, "dve": g.vector, "g": g, "sync": g.sync, "scalar": g.scalar}
    seen, count, log, pending = {}, {"pe": 0, "dve": 0}, [], []

    def ap(t):
        return T[t[0]][:, t[1]:t[2]]

    def need(q, sem, val):
        if seen.get((q, sem), 0) < val:
            Q[q].wait_ge(T.sem[sem], val)
            seen[(q, sem)] = val

    def order(q, reads, writes):
        want = {}
        for is_w, lst in ((False, reads), (True, writes)):
            for buf, lo, hi in lst:
                for b, l, h, w, oq, sem, val in log:
                    if b != buf:
                        continue
                    if buf in PSUM:
                        hit = oq != q
                    else:
                        hit = l < hi and lo < h and ((not is_w and w) or (is_w and oq != q))
                    if hit:
                        want[sem] = max(want.get(sem, 0), val)
        for sem in sorted(want):
            need(q, sem, want[sem])

    def note(q, reads, writes, sem, val):
        for buf, lo, hi in reads:
            log.append((buf, lo, hi, False, q, sem, val))
        for buf, lo, hi in writes:
            log.append((buf, lo, hi, True, q, sem, val))

    def copy(out, in_):
        order("dve", [in_], [out])
        count["dve"] += 1
        g.vector.tensor_copy(ap(out), ap(in_)).then_inc(T.sem.dve, 1)
        note("dve", [in_], [out], "dve", count["dve"])

    def flush(n):
        for ps, sb in pending[:n]:
            copy(sb, ps)
        del pending[:n]

    def mm(out, lhsT, rhs, start, stop):
        n = 0
        for i, (ps, sb) in enumerate(pending):
            if ps[0] == out[0] or any(sb[0] == t[0] and sb[1] < t[2] and t[1] < sb[2] for t in (lhsT, rhs)):
                n = i + 1
        flush(n)
        order("pe", [lhsT, rhs], [out])
        count["pe"] += 1
        g.tensor.matmul(ap(out), ap(lhsT), ap(rhs), start, stop).then_inc(T.sem.pe, 1)
        note("pe", [lhsT, rhs], [out], "pe", count["pe"])

    def add(out, in0, in1):
        order("dve", [in0, in1], [out])
        count["dve"] += 1
        g.vector.tensor_tensor(ap(out), ap(in0), ap(in1), AluOpType.add).then_inc(T.sem.dve, 1)
        note("dve", [in0, in1], [out], "dve", count["dve"])

    def zero(out):
        order("dve", [], [out])
        count["dve"] += 1
        g.vector.memset(ap(out), 0.0).then_inc(T.sem.dve, 1)
        note("dve", [], [out], "dve", count["dve"])

    def load(queue, out, in_, sem):
        queue.dma_start(ap(out), in_).then_inc(T.sem[sem], 16)
        note("dma", [], [out], sem, 16)

    def blk(buf, i, n=1):
        return (buf, i * P, (i + n) * P)

    A1, A2, A3, A6 = blk("q", 0), blk("ap", 0), blk("ap", 1), blk("ap", 2)
    AT1, AT2, AT3, AT6, AT12 = (blk("atp", i) for i in range(5))
    L1, C, V = blk("lc", 0), blk("lc", 1), blk("lc", 2)
    AHEAD = ("xb", S * P - EW, S * P)
    urgent = bool(far[rank])

    if urgent:
        load(g.sync, AHEAD, T.x[:, S * P - EW:S * P], "ldx2")
        load(g.scalar, A1, T.a[:], "lda")
        load(g.sync, ("xb", 0, S * P - EW), T.x[:, 0:S * P - EW], "ldx")
        if rank:
            load(g.sync, AT1, T.at[:], "ldat")
    else:
        load(g.sync, blk("xb", 0, 3), T.x[:], "ldx")
        load(g.scalar, A1, T.a[:], "lda")
        load(g.scalar, AT1, T.at[:], "ldat")

    sources = []
    for j in range(rank):
        if rank in direct[j]:
            sources.append((0, direct[j].index(rank), "land", j))
            note("remote", [], [blk("land", j)], "arr%d" % j, _count(direct_mask(j)))
        else:
            pos = [i for i, (h, r) in enumerate(far[j]) if r == rank][0]
            h = far[j][pos][0]
            n_eng = _count(relay_out_mask(h, [r for hh, r in far[j] if hh == h]))
            sources.append((1, pos, "landx", j))
            sources.append((2, pos, "land", j))
            note("remote", [], [("landx", (j + 1) * P - EW, (j + 1) * P)], "arx%d" % j, n_eng)
            zero(("landx", j * P, (j + 1) * P - EW))
            note("remote", [], [blk("land", j)], "arr%d" % j, n_eng)
    sources.sort()

    tasks = []
    if rank >= 1:
        tasks.append((A2, AT1, A1))
    if rank >= 2:
        tasks = [(AT2, A1, AT1), (A2, AT1, A1), (AT3, A1, AT2)]
        if rank >= 3:
            tasks.append((A3, AT1, A2))
            tasks.append((AT6, A3, AT3))
        tasks.append((blk("q", 1), AT3, A1))
        if rank >= 5:
            tasks.append((A6, AT3, A3))
        if rank >= 3:
            tasks.append((blk("q", 2, min(rank, 4) - 2), AT6, blk("q", 0, min(rank, 4) - 2)))
        if rank >= 5:
            tasks.append((AT12, A6, AT6))
            tasks.append((blk("q", 4, rank - 4), AT12, blk("q", 0, rank - 4)))
    nb = [0]

    def power(t):
        ps = ("pp%d" % (nb[0] % NBANK), 0, t[0][2] - t[0][1])
        nb[0] += 1
        mm(ps, t[1], t[2], True, True)
        pending.append((ps, t[0]))

    mm(("ph", 0, P), A1, blk("xb", 0), True, True)
    if not urgent:
        for t in tasks[:2]:
            power(t)
        tasks = tasks[2:]
    add(L1, ("ph", 0, P), blk("xb", 1))
    flush(len(pending))
    mm(("ph", P, 2 * P), A1, L1, True, True)
    if urgent:
        add(("lc", 2 * P, 3 * P - EW), ("ph", P, 2 * P - EW), ("xb", 2 * P, 3 * P - EW))
        copy(("lc", 3 * P - EW, 3 * P), ("ph", 2 * P - EW, 2 * P))
    add(C, ("ph", P, 2 * P), blk("xb", 2))

    sent = 0
    if far[rank]:
        hs = []
        for h, _r in far[rank]:
            if h not in hs:
                hs.append(h)
        order("g", [AHEAD], [])
        sent += send(ap(AHEAD), hs, relay_in_mask(rank), "landx", "arx", rank, P - EW)
        order("g", [V], [])
        sent += send(ap(V), hs, relay_in_mask(rank), "land", "arr", rank)
    if direct[rank]:
        order("g", [C], [])
        sent += send(ap(C), [cores[r] for r in direct[rank]], direct_mask(rank), "land", "arr", rank)

    for t in tasks:
        power(t)
    flush(len(pending))

    if rank == 0:
        order("sync", [blk("xb", 0)], [])
        g.sync.dma_start(T.y[:, 0:P], ap(blk("xb", 0))).then_inc(T.sem.st, 16)
        order("scalar", [L1, C], [])
        g.scalar.dma_start(T.y[:, P:S * P], T.lc[:, 0:2 * P]).then_inc(T.sem.st2, 16)
        g.sync.wait_ge(T.sem.st, 16)
        g.scalar.wait_ge(T.sem.st2, 16)
    else:
        PH, HB = ("pH", 0, P), ("hb", 0, P)
        for i, (_k, _p, buf, j) in enumerate(sources):
            mm(PH, blk("q", rank - 1 - j), blk(buf, j), i == 0, i == len(sources) - 1)
        copy(HB, PH)
        mm(("py1", 0, P), A1, HB, True, True)
        mm(("py2", 0, P), A2, HB, True, True)
        add(blk("yb", 0), PH, blk("xb", 0))
        add(blk("yb", 1), ("py1", 0, P), L1)
        add(blk("yb", 2), ("py2", 0, P), C)
        order("sync", [blk("yb", 0, 3)], [])
        g.sync.dma_start(T.y[:], T.yb[:]).then_inc(T.sem.st, 16)
        g.sync.wait_ge(T.sem.st, 16)
    if sent:
        g.wait_ge(T.sem.sent, sent)
